import numpy as np
import ml_dtypes


def mxq(x, axis, fmt="e4m3"):
    dtype, down = {"e4m3": (ml_dtypes.float8_e4m3fn, 7), "e5m2": (ml_dtypes.float8_e5m2, 14)}[fmt]
    v = np.moveaxis(np.asarray(x, np.float32).astype(ml_dtypes.bfloat16).astype(np.float64), axis, -1)
    blocks = v.reshape(v.shape[:-1] + (-1, 32))
    amax = np.abs(blocks).max(-1, keepdims=True)
    byte = np.maximum(np.where(amax > 0, np.frexp(amax)[1] - 1 + 127, 0) - down, 1)
    scale = np.exp2(byte - 127.0)
    codes = (blocks / scale).astype(np.float32).astype(dtype).astype(np.float64)
    return np.moveaxis((codes * scale).reshape(v.shape), -1, axis)


WIDE = False


def mx_kscale(k):
    if not WIDE:
        return np.ones(k)
    levels = np.array([10, -10, 5, -5, 0])
    if k % 512:
        return np.exp2(np.random.permutation(np.resize(levels, k // 32))).repeat(32)
    a = np.empty((k // 512, 16))
    for p in range(k // 512):
        a[p, :8] = np.random.permutation(np.resize(levels, 8))
        for g in range(8):
            far = levels[np.abs(levels - a[p, g]) >= 10]
            a[p, g + 8] = far[np.random.randint(len(far))]
    return np.exp2(a.ravel()).repeat(32)


def f64(x):
    return np.asarray(x).astype(np.float64)


def striped(idx):
    return np.tile(np.asarray(idx).reshape(-1, 16).T, (8, 1)).astype(np.uint16)


def unstriped(offs):
    return offs[:16].T.reshape(-1).astype(np.int64)


E2M1 = np.array([0.0, 0.5, 1.0, 1.5, 2.0, 3.0, 4.0, 6.0, -0.0, -0.5, -1.0, -1.5, -2.0, -3.0, -4.0, -6.0])


def pack_weight(w, fmt):
    k, n = w.shape
    w = f64(np.asarray(w, np.float32).astype(ml_dtypes.bfloat16)).reshape(k // 32, 32, n)
    amax = np.abs(w).max(1)
    if fmt == "e4m3":
        byte = np.frexp(amax)[1] - 1 + 127 - 7
    else:
        mant, ex = np.frexp(amax / 6.0)
        byte = np.where(mant > 0.5, ex, ex - 1) + 127
    byte = np.clip(np.where(amax > 0, byte, 1), 1, 254)
    scaled = (w * np.exp2(127.0 - byte)[:, None, :]).reshape(k, n).astype(np.float32)
    by_word = np.ascontiguousarray(scaled.reshape(k // 512, 128, 4, n).transpose(0, 1, 3, 2))
    if fmt == "e4m3":
        words = by_word.astype(ml_dtypes.float8_e4m3fn).view(np.uint8)
    else:
        c = by_word.astype(ml_dtypes.float4_e2m1fn).view(np.uint8) & 0xF
        words = (c[..., 0::2] | (c[..., 1::2] << 4)).reshape(k // 512, 128, 2 * n)
    return np.ascontiguousarray(words), np.ascontiguousarray(byte.astype(np.uint8).reshape(k // 512, 16, n))


def unpack_weight(words, scales, fmt):
    g, _, n = scales.shape
    words = np.ascontiguousarray(words).reshape(g, 128, n, -1)
    if fmt == "e4m3":
        vals = words.view(ml_dtypes.float8_e4m3fn).astype(np.float64)
    else:
        nib = np.empty((g, 128, n, 4), np.uint8)
        nib[..., 0::2] = words & 0xF
        nib[..., 1::2] = words >> 4
        vals = E2M1[nib]
    vals = vals * np.repeat(np.exp2(scales.astype(np.float64) - 127.0), 8, axis=1)[..., None]
    return vals.transpose(0, 1, 3, 2).reshape(g * 512, n)


def sigmoid(v):
    return 1.0 / (1.0 + np.exp(-v))


B, N, T, D, NQ = 1, 512, 2048, 512, 512
SEG = 16


def setup_inputs():
    n = np.random.standard_normal
    idx = np.random.permutation(T)[:B * N]
    s = mx_kscale(D)[:, None]
    kp = pack_weight(n((D, T)) / s, "e4m3")
    return {
        "qT": (n((B, D, NQ)) * s * (1.00 / np.sqrt(D))).astype(np.float32),
        "k_words": kp[0],
        "k_scales": kp[1],
        "hw": (np.random.uniform(-0.5, 1.0, (B, 1, NQ))).astype(np.float32),
        "offs": striped(idx),
    }


def reference(qT, k_words, k_scales, hw, offs):
    idx = unstriped(offs)
    pick = lambda x, which: x[:, which].reshape(x.shape[0], B, -1).transpose(1, 0, 2)
    k = unpack_weight(k_words, k_scales, "e4m3")
    kg = pick(k, idx)
    qq = mxq(f64(qT), 1, "e4m3")
    a = kg.transpose(0, 2, 1) @ qq
    y = (sigmoid(a) * f64(hw)).reshape(B, N, NQ // SEG, SEG).sum(-1)
    return y

@@ -1,0 +1,174 @@
+from contextlib import ExitStack
+
+import concourse.mybir as mybir
+from concourse.masks import make_identity
+
+F32 = mybir.dt.float32
+BF16 = mybir.dt.bfloat16
+I32 = mybir.dt.int32
+U32 = mybir.dt.uint32
+U16 = mybir.dt.uint16
+U8 = mybir.dt.uint8
+FP8X4 = mybir.dt.float8_e4m3fn_x4
+MULT = mybir.AluOpType.mult
+ADD = mybir.AluOpType.add
+SIGMOID = mybir.ActivationFunctionType.Sigmoid
+COPY = mybir.ActivationFunctionType.Copy
+
+P = 128
+PACK = 4
+N, T, D, NQ, SEG = 512, 2048, 512, 512, 16
+NJ = NQ // SEG
+QT = NQ // P
+HALF = 256
+M_VECTOR = 64
+LAST_PIECES = [(0, 64), (64, 128)]
+
+FLOPS = 2 * N * D * NQ
+
+
+def tile_attend_tok_sigidx_topk_kernel(tc, qT, k_words, k_scales, hw, offs, out):
+    nc = tc.nc
+    with ExitStack() as ctx:
+        keep = ctx.enter_context(tc.tile_pool(name="keep", bufs=1))
+        psum = ctx.enter_context(tc.psum_pool(name="psum", bufs=1))
+
+        offsets = keep.tile([P, N // 16], U16, name="offsets")
+        q_raw = keep.tile([P, PACK, NQ], F32, name="q_raw", align_bytes=64)
+        pool_words = keep.tile([P, T], U32, name="pool_words", align_bytes=64)
+        pool_scales = keep.tile([P, T], U8, name="pool_scales", align_bytes=64)
+        hw_col = keep.tile([P, QT], F32, name="hw_col")
+        ident = keep.tile([P, P], F32, name="ident", align_bytes=64)
+        warm = keep.tile([P, 8], F32, name="warm")
+
+        nc.gpsimd.memset(pool_scales[:].bitcast(I32), 0)
+        for quad in (0, 2, 1, 3):
+            nc.sync.dma_start(
+                out=pool_scales[32 * quad : 32 * quad + 4, :].bitcast(I32),
+                in_=k_scales[0, 4 * quad : 4 * quad + 4, :].bitcast(I32),
+            )
+        nc.sync.dma_start(offsets[:], offs)
+        nc.sync.dma_start(out=q_raw[:], in_=qT[0].rearrange("(p r) q -> p r q", r=PACK))
+        nc.scalar.dma_start(out=hw_col[:], in_=hw[0, 0].rearrange("(p t) -> p t", t=QT))
+        nc.sync.dma_start(
+            out=pool_words[:].bitcast(I32),
+            in_=k_words[0].rearrange("p t r -> p (t r)").bitcast(I32),
+        )
+
+        nc.vector.memset(warm[:], 0.0)
+        nc.scalar.activation(warm[:], warm[:], SIGMOID)
+        make_identity(nc, ident[:])
+
+        key_scales = keep.tile([P, N], U8, name="key_scales", align_bytes=64)
+        nc.vector.tensor_copy(key_scales[:], pool_scales[:].indirect(offsets[:]))
+
+        q_bf = keep.tile([P, QT, P, PACK], BF16, name="q_bf", align_bytes=64)
+        src = q_raw[:].rearrange("p r (m t) -> p m t r", t=QT)
+        dst = q_bf[:].rearrange("p t m r -> p m t r")
+        nc.scalar.activation(dst[:, M_VECTOR:P], src[:, M_VECTOR:P], COPY)
+        nc.vector.tensor_copy(dst[:, 0:M_VECTOR], src[:, 0:M_VECTOR])
+
+        q_words = keep.tile([P, NQ], U32, name="q_words", align_bytes=64)
+        q_scales = keep.tile([P, NQ], U8, name="q_scales", align_bytes=64)
+        nc.vector.quantize_mx(
+            out=q_words[:].bitcast(FP8X4),
+            scales=q_scales[:],
+            in_=q_bf[:].rearrange("p t m r -> p (t m r)"),
+        )
+
+        key_words = []
+        for h in range(2):
+            words = keep.tile([P, HALF], U32, name="key_words%d" % h, align_bytes=64)
+            nc.vector.tensor_copy(words[:], pool_words[:].indirect(offsets[:, 16 * h : 16 * (h + 1)]))
+            key_words.append(words)
+
+        hw_row = psum.tile([P, QT, P], F32, name="hw_row")
+        for t in range(QT):
+            nc.tensor.transpose(hw_row[:, t, :], hw_col[:, t : t + 1].to_broadcast([P, P]), ident[:])
+
+        def mx(bank, rows, rows_scale, cols, cols_scale):
+            nc.tensor.matmul_mx(
+                out=bank,
+                lhsT=rows.bitcast(FP8X4),
+                lhsT_scale=rows_scale,
+                rhs=cols.bitcast(FP8X4),
+                rhs_scale=cols_scale,
+                start=True,
+                stop=True,
+            )
+
+        turned = [psum.tile([P, P], F32, name="turned%d" % kb) for kb in range(3)]
+        res = [keep.tile([P, 2, NJ], F32, name="res%d" % h) for h in range(2)]
+        out_rows = out[0].rearrange("(h kb p) j -> h p kb j", h=2, p=P)
+
+        def weigh_and_turn(name, sigs, blocks):
+            width = P * len(blocks)
+            for pair in range(2):
+                t0, t1 = 2 * pair, 2 * pair + 1
+                first = keep.tile([P, width], F32, name="first%s_%d" % (name, pair), align_bytes=64)
+                both = keep.tile([P, width], F32, name="both%s_%d" % (name, pair), align_bytes=64)
+                nc.vector.tensor_scalar(first[:], sigs[t0], hw_col[:, t0 : t0 + 1], None, MULT)
+                nc.vector.scalar_tensor_tensor(both[:], sigs[t1], hw_col[:, t1 : t1 + 1], first[:], MULT, ADD)
+                for i, kb in enumerate(blocks):
+                    nc.tensor.matmul(
+                        turned[kb][:],
+                        lhsT=both[:, P * i : P * (i + 1)],
+                        rhs=ident[:],
+                        start=(pair == 0),
+                        stop=(pair == 1),
+                        is_transpose=True,
+                    )
+
+        def sum_turned(kb):
+            nc.vector.tensor_reduce(
+                res[kb // 2][:, kb % 2, :],
+                turned[kb][:].rearrange("p (j g) -> p j g", g=4),
+                mybir.AxisListType.X,
+                ADD,
+            )
+
+        sig_a = []
+        for t in range(QT):
+            bank = psum.tile([P, HALF], F32, name="score_a%d" % t, tag="score%d" % t)
+            mx(bank[:], q_words[:, P * t : P * (t + 1)], q_scales[:, P * t : P * (t + 1)],
+               key_words[0][:], key_scales[:, 0:HALF])
+            sig = keep.tile([P, HALF], F32, name="sig_a%d" % t, align_bytes=64)
+            nc.scalar.activation(sig[:], bank[:], SIGMOID)
+            sig_a.append(sig[:])
+
+        sig_b = []
+        for pair in range(2):
+            bank = psum.tile([P, 2, P], F32, name="score_b%d" % pair, tag="score%d" % pair)
+            for i in range(2):
+                t = 2 * pair + i
+                mx(bank[:, i, :], q_words[:, P * t : P * (t + 1)], q_scales[:, P * t : P * (t + 1)],
+                   key_words[1][:, 0:P], key_scales[:, 2 * P : 3 * P])
+            sig = keep.tile([P, 2, P], F32, name="sig_b%d" % pair, align_bytes=64)
+            nc.scalar.activation(sig[:], bank[:], SIGMOID)
+            sig_b.extend([sig[:, 0, :], sig[:, 1, :]])
+
+        bank_c = psum.tile([P, QT, P], F32, name="score_c", tag="score2")
+        mx(bank_c[:].rearrange("p t m -> p (t m)"), key_words[1][:, P:HALF], key_scales[:, 3 * P : N],
+           q_words[:], q_scales[:])
+        sig_c = keep.tile([P, QT, P], F32, name="sig_c", align_bytes=64)
+        for lo, hi in LAST_PIECES:
+            nc.scalar.activation(sig_c[:, :, lo:hi], bank_c[:, :, lo:hi], SIGMOID)
+
+        weigh_and_turn("a", sig_a, [0, 1])
+        weigh_and_turn("b", sig_b, [2])
+        sum_turned(0)
+        sum_turned(1)
+        nc.sync.dma_start(out=out_rows[0], in_=res[0][:])
+
+        prod = keep.tile([P, QT, P], F32, name="prod", align_bytes=64)
+        for lo, hi in LAST_PIECES:
+            nc.vector.tensor_tensor(prod[:, :, lo:hi], sig_c[:, :, lo:hi], hw_row[:, :, lo:hi], MULT)
+        sum_turned(2)
+        for lo, hi in LAST_PIECES:
+            nc.vector.tensor_reduce(
+                res[1][:, 1, lo // 4 : hi // 4],
+                prod[:, :, lo:hi].rearrange("p t (j g) -> p j t g", g=4),
+                mybir.AxisListType.XY,
+                ADD,
+            )
+        nc.sync.dma_start(out=out_rows[1], in_=res[1][:])

@@ -22,7 +22,8 @@ NJ = NQ // SEG
 QT = NQ // P
 HALF = 256
 M_VECTOR = 64
-LAST_PIECES = [(0, 64), (64, 128)]
+SCORE_BANKS = 5
+SLOT = 12
 
 FLOPS = 2 * N * D * NQ
 
@@ -42,13 +43,13 @@ def tile_attend_tok_sigidx_topk_kernel(tc, qT, k_words, k_scales, hw, offs, out)
         warm = keep.tile([P, 8], F32, name="warm")
 
         nc.gpsimd.memset(pool_scales[:].bitcast(I32), 0)
+        nc.sync.dma_start(out=q_raw[:], in_=qT[0].rearrange("(p r) q -> p r q", r=PACK))
+        nc.sync.dma_start(offsets[:], offs)
         for quad in (0, 2, 1, 3):
             nc.sync.dma_start(
                 out=pool_scales[32 * quad : 32 * quad + 4, :].bitcast(I32),
                 in_=k_scales[0, 4 * quad : 4 * quad + 4, :].bitcast(I32),
             )
-        nc.sync.dma_start(offsets[:], offs)
-        nc.sync.dma_start(out=q_raw[:], in_=qT[0].rearrange("(p r) q -> p r q", r=PACK))
         nc.scalar.dma_start(out=hw_col[:], in_=hw[0, 0].rearrange("(p t) -> p t", t=QT))
         nc.sync.dma_start(
             out=pool_words[:].bitcast(I32),
@@ -82,9 +83,15 @@ def tile_attend_tok_sigidx_topk_kernel(tc, qT, k_words, k_scales, hw, offs, out)
             nc.vector.tensor_copy(words[:], pool_words[:].indirect(offsets[:, 16 * h : 16 * (h + 1)]))
             key_words.append(words)
 
-        hw_row = psum.tile([P, QT, P], F32, name="hw_row")
-        for t in range(QT):
-            nc.tensor.transpose(hw_row[:, t, :], hw_col[:, t : t + 1].to_broadcast([P, P]), ident[:])
+        bank_x = psum.tile([P, 3, P], F32, name="bank_x")
+        bank_y = psum.tile([P, 2, P], F32, name="bank_y")
+        bank_z = psum.tile([P, P], F32, name="bank_z")
+        hw_row = bank_x[:, 1:3, :]
+        turned = {0: bank_x[:, 0, :], 1: bank_y[:, 0, :], 3: bank_y[:, 1, :], 2: bank_z[:]}
+        for i in range(2):
+            nc.tensor.transpose(hw_row[:, i, :], hw_col[:, 2 + i : 3 + i].to_broadcast([P, P]), ident[:])
+
+        sigs = []
 
         def mx(bank, rows, rows_scale, cols, cols_scale):
             nc.tensor.matmul_mx(
@@ -97,78 +104,89 @@ def tile_attend_tok_sigidx_topk_kernel(tc, qT, k_words, k_scales, hw, offs, out)
                 stop=True,
             )
 
-        turned = [psum.tile([P, P], F32, name="turned%d" % kb) for kb in range(3)]
-        res = [keep.tile([P, 2, NJ], F32, name="res%d" % h) for h in range(2)]
-        out_rows = out[0].rearrange("(h kb p) j -> h p kb j", h=2, p=P)
+        def block_words(kb):
+            return key_words[kb // 2][:, P * (kb % 2) : P * (kb % 2 + 1)]
 
-        def weigh_and_turn(name, sigs, blocks):
-            width = P * len(blocks)
-            for pair in range(2):
-                t0, t1 = 2 * pair, 2 * pair + 1
-                first = keep.tile([P, width], F32, name="first%s_%d" % (name, pair), align_bytes=64)
-                both = keep.tile([P, width], F32, name="both%s_%d" % (name, pair), align_bytes=64)
-                nc.vector.tensor_scalar(first[:], sigs[t0], hw_col[:, t0 : t0 + 1], None, MULT)
-                nc.vector.scalar_tensor_tensor(both[:], sigs[t1], hw_col[:, t1 : t1 + 1], first[:], MULT, ADD)
-                for i, kb in enumerate(blocks):
-                    nc.tensor.matmul(
-                        turned[kb][:],
-                        lhsT=both[:, P * i : P * (i + 1)],
-                        rhs=ident[:],
-                        start=(pair == 0),
-                        stop=(pair == 1),
-                        is_transpose=True,
-                    )
+        def block_scales(kb):
+            return key_scales[:, P * kb : P * (kb + 1)]
 
-        def sum_turned(kb):
-            nc.vector.tensor_reduce(
-                res[kb // 2][:, kb % 2, :],
-                turned[kb][:].rearrange("p (j g) -> p j g", g=4),
-                mybir.AxisListType.X,
-                ADD,
-            )
+        def new_bank():
+            i = len(sigs)
+            return psum.tile([P, 2, P], F32, name="score%d" % i, tag="score%d" % (i % SCORE_BANKS))
 
-        sig_a = []
-        for t in range(QT):
-            bank = psum.tile([P, HALF], F32, name="score_a%d" % t, tag="score%d" % t)
-            mx(bank[:], q_words[:, P * t : P * (t + 1)], q_scales[:, P * t : P * (t + 1)],
-               key_words[0][:], key_scales[:, 0:HALF])
-            sig = keep.tile([P, HALF], F32, name="sig_a%d" % t, align_bytes=64)
+        def sigmoid(bank):
+            sig = keep.tile([P, 2, P], F32, name="sig%d" % len(sigs), align_bytes=64)
             nc.scalar.activation(sig[:], bank[:], SIGMOID)
-            sig_a.append(sig[:])
+            sigs.append(sig)
+            return sig
 
-        sig_b = []
-        for pair in range(2):
-            bank = psum.tile([P, 2, P], F32, name="score_b%d" % pair, tag="score%d" % pair)
+        def by_query(kb, t0):
+            bank = new_bank()
             for i in range(2):
-                t = 2 * pair + i
-                mx(bank[:, i, :], q_words[:, P * t : P * (t + 1)], q_scales[:, P * t : P * (t + 1)],
-                   key_words[1][:, 0:P], key_scales[:, 2 * P : 3 * P])
-            sig = keep.tile([P, 2, P], F32, name="sig_b%d" % pair, align_bytes=64)
-            nc.scalar.activation(sig[:], bank[:], SIGMOID)
-            sig_b.extend([sig[:, 0, :], sig[:, 1, :]])
+                cols = slice(P * (t0 + i), P * (t0 + i + 1))
+                mx(bank[:, i, :], q_words[:, cols], q_scales[:, cols], block_words(kb), block_scales(kb))
+            return sigmoid(bank)
 
-        bank_c = psum.tile([P, QT, P], F32, name="score_c", tag="score2")
-        mx(bank_c[:].rearrange("p t m -> p (t m)"), key_words[1][:, P:HALF], key_scales[:, 3 * P : N],
-           q_words[:], q_scales[:])
-        sig_c = keep.tile([P, QT, P], F32, name="sig_c", align_bytes=64)
-        for lo, hi in LAST_PIECES:
-            nc.scalar.activation(sig_c[:, :, lo:hi], bank_c[:, :, lo:hi], SIGMOID)
+        def by_key(kb):
+            bank = new_bank()
+            mx(bank[:].rearrange("p t m -> p (t m)"), block_words(kb), block_scales(kb),
+               q_words[:, 2 * P : NQ], q_scales[:, 2 * P : NQ])
+            return sigmoid(bank)
 
-        weigh_and_turn("a", sig_a, [0, 1])
-        weigh_and_turn("b", sig_b, [2])
-        sum_turned(0)
-        sum_turned(1)
+        def weigh(kb, sig):
+            low = keep.tile([P, 2, P], F32, name="low%d" % kb, align_bytes=64)
+            for i in range(2):
+                nc.vector.tensor_scalar(low[:, i, :], sig[:, i, :], hw_col[:, i : i + 1], None, MULT)
+            return low
+
+        def weigh_onto(kb, sig, low):
+            both = keep.tile([P, 2, P], F32, name="both%d" % kb, align_bytes=64)
+            for i in range(2):
+                nc.vector.scalar_tensor_tensor(
+                    both[:, i, :], sig[:, i, :], hw_col[:, 2 + i : 3 + i], low[:, i, :], MULT, ADD
+                )
+            return both
+
+        def turn(kb, sums):
+            for i in range(2):
+                nc.tensor.matmul(
+                    turned[kb], lhsT=sums[:, i, :], rhs=ident[:], start=(i == 0), stop=(i == 1), is_transpose=True
+                )
+
+        def sum_turned(dest, kb):
+            nc.vector.tensor_reduce(dest, turned[kb].rearrange("p (j g) -> p j g", g=4), mybir.AxisListType.X, ADD)
+
+        s00, s01 = by_query(0, 0), by_query(0, 2)
+        s10, s11 = by_query(1, 0), by_query(1, 2)
+        s30 = by_query(3, 0)
+        s20, s21 = by_query(2, 0), by_query(2, 2)
+        s31 = by_key(3)
+
+        res = [keep.tile([P, NJ], F32, name="res%d" % kb) for kb in range(4)]
+        out_rows = out[0].rearrange("(kb p) j -> kb p j", p=P)
+        terms = keep.tile([P, NJ, SLOT], F32, name="terms", align_bytes=64)
+
+        sums0 = weigh_onto(0, s01, weigh(0, s00))
+        sums1 = weigh_onto(1, s11, weigh(1, s10))
+        sums3 = weigh(3, s30)
+        low2 = weigh(2, s20)
+        turn(0, sums0)
+        turn(1, sums1)
+        turn(3, sums3)
+        sum_turned(res[0][:], 0)
         nc.sync.dma_start(out=out_rows[0], in_=res[0][:])
-
-        prod = keep.tile([P, QT, P], F32, name="prod", align_bytes=64)
-        for lo, hi in LAST_PIECES:
-            nc.vector.tensor_tensor(prod[:, :, lo:hi], sig_c[:, :, lo:hi], hw_row[:, :, lo:hi], MULT)
-        sum_turned(2)
-        for lo, hi in LAST_PIECES:
-            nc.vector.tensor_reduce(
-                res[1][:, 1, lo // 4 : hi // 4],
-                prod[:, :, lo:hi].rearrange("p t (j g) -> p j t g", g=4),
-                mybir.AxisListType.XY,
-                ADD,
-            )
+        sums2 = weigh_onto(2, s21, low2)
+        turn(2, sums2)
+        nc.vector.tensor_tensor(
+            terms[:, :, 0:8].rearrange("p j (t g) -> p t j g", t=2),
+            s31[:].rearrange("p t (j g) -> p t j g", g=4),
+            hw_row.rearrange("p t (j g) -> p t j g", g=4),
+            MULT,
+        )
+        sum_turned(terms[:, :, 8], 3)
+        sum_turned(res[1][:], 1)
         nc.sync.dma_start(out=out_rows[1], in_=res[1][:])
+        nc.vector.tensor_reduce(res[3][:], terms[:, :, 0:9], mybir.AxisListType.X, ADD)
+        nc.scalar.dma_start(out=out_rows[3], in_=res[3][:])
+        sum_turned(res[2][:], 2)
+        nc.sync.dma_start(out=out_rows[2], in_=res[2][:])

@@ -21,7 +21,7 @@ N, T, D, NQ, SEG = 512, 2048, 512, 512, 16
 NJ = NQ // SEG
 QT = NQ // P
 HALF = 256
-M_VECTOR = 64
+M_VECTOR = 52
 SCORE_BANKS = 5
 SLOT = 12
 
@@ -37,7 +37,7 @@ def tile_attend_tok_sigidx_topk_kernel(tc, qT, k_words, k_scales, hw, offs, out)
         offsets = keep.tile([P, N // 16], U16, name="offsets")
         q_raw = keep.tile([P, PACK, NQ], F32, name="q_raw", align_bytes=64)
         pool_words = keep.tile([P, T], U32, name="pool_words", align_bytes=64)
-        pool_scales = keep.tile([P, T], U8, name="pool_scales", align_bytes=64)
+        pool_scales = keep.tile([P, T], U8, name="pool_scales", tag="scales_then_words", align_bytes=64)
         hw_col = keep.tile([P, QT], F32, name="hw_col")
         ident = keep.tile([P, P], F32, name="ident", align_bytes=64)
         warm = keep.tile([P, 8], F32, name="warm")
@@ -69,7 +69,7 @@ def tile_attend_tok_sigidx_topk_kernel(tc, qT, k_words, k_scales, hw, offs, out)
         nc.scalar.activation(dst[:, M_VECTOR:P], src[:, M_VECTOR:P], COPY)
         nc.vector.tensor_copy(dst[:, 0:M_VECTOR], src[:, 0:M_VECTOR])
 
-        q_words = keep.tile([P, NQ], U32, name="q_words", align_bytes=64)
+        q_words = keep.tile([P, NQ], U32, name="q_words", tag="scales_then_words", align_bytes=64)
         q_scales = keep.tile([P, NQ], U8, name="q_scales", align_bytes=64)
         nc.vector.quantize_mx(
             out=q_words[:].bitcast(FP8X4),

@@ -114,18 +114,22 @@ def tile_attend_tok_sigidx_topk_kernel(tc, qT, k_words, k_scales, hw, offs, out)
             i = len(sigs)
             return psum.tile([P, 2, P], F32, name="score%d" % i, tag="score%d" % (i % SCORE_BANKS))
 
-        def sigmoid(bank):
+        def sigmoid(bank, apart=False):
             sig = keep.tile([P, 2, P], F32, name="sig%d" % len(sigs), align_bytes=64)
-            nc.scalar.activation(sig[:], bank[:], SIGMOID)
+            if apart:
+                for i in range(2):
+                    nc.scalar.activation(sig[:, i, :], bank[:, i, :], SIGMOID)
+            else:
+                nc.scalar.activation(sig[:], bank[:], SIGMOID)
             sigs.append(sig)
             return sig
 
-        def by_query(kb, t0):
+        def by_query(kb, t0, apart=False):
             bank = new_bank()
             for i in range(2):
                 cols = slice(P * (t0 + i), P * (t0 + i + 1))
                 mx(bank[:, i, :], q_words[:, cols], q_scales[:, cols], block_words(kb), block_scales(kb))
-            return sigmoid(bank)
+            return sigmoid(bank, apart)
 
         def by_key(kb):
             bank = new_bank()
@@ -159,7 +163,7 @@ def tile_attend_tok_sigidx_topk_kernel(tc, qT, k_words, k_scales, hw, offs, out)
         s00, s01 = by_query(0, 0), by_query(0, 2)
         s10, s11 = by_query(1, 0), by_query(1, 2)
         s30 = by_query(3, 0)
-        s20, s21 = by_query(2, 0), by_query(2, 2)
+        s20, s21 = by_query(2, 0), by_query(2, 2, True)
         s31 = by_key(3)
 
         res = [keep.tile([P, NJ], F32, name="res%d" % kb) for kb in range(4)]
@@ -168,11 +172,14 @@ def tile_attend_tok_sigidx_topk_kernel(tc, qT, k_words, k_scales, hw, offs, out)
 
         sums0 = weigh_onto(0, s01, weigh(0, s00))
         sums1 = weigh_onto(1, s11, weigh(1, s10))
-        sums3 = weigh(3, s30)
+        first3 = keep.tile([P, P], F32, name="first3", align_bytes=64)
+        sum3 = keep.tile([P, P], F32, name="sum3", align_bytes=64)
+        nc.vector.tensor_scalar(first3[:], s30[:, 0, :], hw_col[:, 0:1], None, MULT)
+        nc.vector.scalar_tensor_tensor(sum3[:], s30[:, 1, :], hw_col[:, 1:2], first3[:], MULT, ADD)
         low2 = weigh(2, s20)
         turn(0, sums0)
         turn(1, sums1)
-        turn(3, sums3)
+        nc.tensor.transpose(turned[3], sum3[:], ident[:])
         sum_turned(res[0][:], 0)
         nc.sync.dma_start(out=out_rows[0], in_=res[0][:])
         sums2 = weigh_onto(2, s21, low2)

from contextlib import ExitStack

import concourse.mybir as mybir
from concourse.masks import make_identity

F32 = mybir.dt.float32
BF16 = mybir.dt.bfloat16
I32 = mybir.dt.int32
U32 = mybir.dt.uint32
U16 = mybir.dt.uint16
U8 = mybir.dt.uint8
FP8X4 = mybir.dt.float8_e4m3fn_x4
MULT = mybir.AluOpType.mult
ADD = mybir.AluOpType.add
SIGMOID = mybir.ActivationFunctionType.Sigmoid
COPY = mybir.ActivationFunctionType.Copy

P = 128
PACK = 4
N, T, D, NQ, SEG = 512, 2048, 512, 512, 16
NJ = NQ // SEG
QT = NQ // P
HALF = 256
M_VECTOR = 52
SCORE_BANKS = 5
SLOT = 12

FLOPS = 2 * N * D * NQ


def tile_attend_tok_sigidx_topk_kernel(tc, qT, k_words, k_scales, hw, offs, out):
    nc = tc.nc
    with ExitStack() as ctx:
        keep = ctx.enter_context(tc.tile_pool(name="keep", bufs=1))
        psum = ctx.enter_context(tc.psum_pool(name="psum", bufs=1))

        offsets = keep.tile([P, N // 16], U16, name="offsets")
        q_raw = keep.tile([P, PACK, NQ], F32, name="q_raw", align_bytes=64)
        pool_words = keep.tile([P, T], U32, name="pool_words", align_bytes=64)
        pool_scales = keep.tile([P, T], U8, name="pool_scales", tag="scales_then_words", align_bytes=64)
        hw_col = keep.tile([P, QT], F32, name="hw_col")
        ident = keep.tile([P, P], F32, name="ident", align_bytes=64)
        warm = keep.tile([P, 8], F32, name="warm")

        nc.gpsimd.memset(pool_scales[:].bitcast(I32), 0)
        nc.sync.dma_start(out=q_raw[:], in_=qT[0].rearrange("(p r) q -> p r q", r=PACK))
        nc.sync.dma_start(offsets[:], offs)
        for quad in (0, 2, 1, 3):
            nc.sync.dma_start(
                out=pool_scales[32 * quad : 32 * quad + 4, :].bitcast(I32),
                in_=k_scales[0, 4 * quad : 4 * quad + 4, :].bitcast(I32),
            )
        nc.scalar.dma_start(out=hw_col[:], in_=hw[0, 0].rearrange("(p t) -> p t", t=QT))
        nc.sync.dma_start(
            out=pool_words[:].bitcast(I32),
            in_=k_words[0].rearrange("p t r -> p (t r)").bitcast(I32),
        )

        nc.vector.memset(warm[:], 0.0)
        nc.scalar.activation(warm[:], warm[:], SIGMOID)
        make_identity(nc, ident[:])

        key_scales = keep.tile([P, N], U8, name="key_scales", align_bytes=64)
        nc.vector.tensor_copy(key_scales[:], pool_scales[:].indirect(offsets[:]))

        q_bf = keep.tile([P, QT, P, PACK], BF16, name="q_bf", align_bytes=64)
        src = q_raw[:].rearrange("p r (m t) -> p m t r", t=QT)
        dst = q_bf[:].rearrange("p t m r -> p m t r")
        nc.scalar.activation(dst[:, M_VECTOR:P], src[:, M_VECTOR:P], COPY)
        nc.vector.tensor_copy(dst[:, 0:M_VECTOR], src[:, 0:M_VECTOR])

        q_words = keep.tile([P, NQ], U32, name="q_words", tag="scales_then_words", align_bytes=64)
        q_scales = keep.tile([P, NQ], U8, name="q_scales", align_bytes=64)
        nc.vector.quantize_mx(
            out=q_words[:].bitcast(FP8X4),
            scales=q_scales[:],
            in_=q_bf[:].rearrange("p t m r -> p (t m r)"),
        )

        key_words = []
        for h in range(2):
            words = keep.tile([P, HALF], U32, name="key_words%d" % h, align_bytes=64)
            nc.vector.tensor_copy(words[:], pool_words[:].indirect(offsets[:, 16 * h : 16 * (h + 1)]))
            key_words.append(words)

        bank_x = psum.tile([P, 3, P], F32, name="bank_x")
        bank_y = psum.tile([P, 2, P], F32, name="bank_y")
        bank_z = psum.tile([P, P], F32, name="bank_z")
        hw_row = bank_x[:, 1:3, :]
        turned = {0: bank_x[:, 0, :], 1: bank_y[:, 0, :], 3: bank_y[:, 1, :], 2: bank_z[:]}
        for i in range(2):
            nc.tensor.transpose(hw_row[:, i, :], hw_col[:, 2 + i : 3 + i].to_broadcast([P, P]), ident[:])

        sigs = []

        def mx(bank, rows, rows_scale, cols, cols_scale):
            nc.tensor.matmul_mx(
                out=bank,
                lhsT=rows.bitcast(FP8X4),
                lhsT_scale=rows_scale,
                rhs=cols.bitcast(FP8X4),
                rhs_scale=cols_scale,
                start=True,
                stop=True,
            )

        def block_words(kb):
            return key_words[kb // 2][:, P * (kb % 2) : P * (kb % 2 + 1)]

        def block_scales(kb):
            return key_scales[:, P * kb : P * (kb + 1)]

        def new_bank():
            i = len(sigs)
            return psum.tile([P, 2, P], F32, name="score%d" % i, tag="score%d" % (i % SCORE_BANKS))

        def sigmoid(bank, apart=False):
            sig = keep.tile([P, 2, P], F32, name="sig%d" % len(sigs), align_bytes=64)
            if apart:
                for i in range(2):
                    nc.scalar.activation(sig[:, i, :], bank[:, i, :], SIGMOID)
            else:
                nc.scalar.activation(sig[:], bank[:], SIGMOID)
            sigs.append(sig)
            return sig

        def by_query(kb, t0, apart=False):
            bank = new_bank()
            for i in range(2):
                cols = slice(P * (t0 + i), P * (t0 + i + 1))
                mx(bank[:, i, :], q_words[:, cols], q_scales[:, cols], block_words(kb), block_scales(kb))
            return sigmoid(bank, apart)

        def by_key(kb):
            bank = new_bank()
            mx(bank[:].rearrange("p t m -> p (t m)"), block_words(kb), block_scales(kb),
               q_words[:, 2 * P : NQ], q_scales[:, 2 * P : NQ])
            return sigmoid(bank)

        def weigh(kb, sig):
            low = keep.tile([P, 2, P], F32, name="low%d" % kb, align_bytes=64)
            for i in range(2):
                nc.vector.tensor_scalar(low[:, i, :], sig[:, i, :], hw_col[:, i : i + 1], None, MULT)
            return low

        def weigh_onto(kb, sig, low):
            both = keep.tile([P, 2, P], F32, name="both%d" % kb, align_bytes=64)
            for i in range(2):
                nc.vector.scalar_tensor_tensor(
                    both[:, i, :], sig[:, i, :], hw_col[:, 2 + i : 3 + i], low[:, i, :], MULT, ADD
                )
            return both

        def turn(kb, sums):
            for i in range(2):
                nc.tensor.matmul(
                    turned[kb], lhsT=sums[:, i, :], rhs=ident[:], start=(i == 0), stop=(i == 1), is_transpose=True
                )

        def sum_turned(dest, kb):
            nc.vector.tensor_reduce(dest, turned[kb].rearrange("p (j g) -> p j g", g=4), mybir.AxisListType.X, ADD)

        s00, s01 = by_query(0, 0), by_query(0, 2)
        s10, s11 = by_query(1, 0), by_query(1, 2)
        s30 = by_query(3, 0)
        s20, s21 = by_query(2, 0), by_query(2, 2, True)
        s31 = by_key(3)

        res = [keep.tile([P, NJ], F32, name="res%d" % kb) for kb in range(4)]
        out_rows = out[0].rearrange("(kb p) j -> kb p j", p=P)
        terms = keep.tile([P, NJ, SLOT], F32, name="terms", align_bytes=64)

        sums0 = weigh_onto(0, s01, weigh(0, s00))
        sums1 = weigh_onto(1, s11, weigh(1, s10))
        first3 = keep.tile([P, P], F32, name="first3", align_bytes=64)
        sum3 = keep.tile([P, P], F32, name="sum3", align_bytes=64)
        nc.vector.tensor_scalar(first3[:], s30[:, 0, :], hw_col[:, 0:1], None, MULT)
        nc.vector.scalar_tensor_tensor(sum3[:], s30[:, 1, :], hw_col[:, 1:2], first3[:], MULT, ADD)
        low2 = weigh(2, s20)
        turn(0, sums0)
        turn(1, sums1)
        nc.tensor.transpose(turned[3], sum3[:], ident[:])
        sum_turned(res[0][:], 0)
        nc.sync.dma_start(out=out_rows[0], in_=res[0][:])
        sums2 = weigh_onto(2, s21, low2)
        turn(2, sums2)
        nc.vector.tensor_tensor(
            terms[:, :, 0:8].rearrange("p j (t g) -> p t j g", t=2),
            s31[:].rearrange("p t (j g) -> p t j g", g=4),
            hw_row.rearrange("p t (j g) -> p t j g", g=4),
            MULT,
        )
        sum_turned(terms[:, :, 8], 3)
        sum_turned(res[1][:], 1)
        nc.sync.dma_start(out=out_rows[1], in_=res[1][:])
        nc.vector.tensor_reduce(res[3][:], terms[:, :, 0:9], mybir.AxisListType.X, ADD)
        nc.scalar.dma_start(out=out_rows[3], in_=res[3][:])
        sum_turned(res[2][:], 2)
        nc.sync.dma_start(out=out_rows[2], in_=res[2][:])
